import numpy as np
import ml_dtypes


def mxq(x, axis, fmt="e4m3"):
    dtype, down = {"e4m3": (ml_dtypes.float8_e4m3fn, 7), "e5m2": (ml_dtypes.float8_e5m2, 14)}[fmt]
    v = np.moveaxis(np.asarray(x, np.float32).astype(ml_dtypes.bfloat16).astype(np.float64), axis, -1)
    blocks = v.reshape(v.shape[:-1] + (-1, 32))
    amax = np.abs(blocks).max(-1, keepdims=True)
    byte = np.maximum(np.where(amax > 0, np.frexp(amax)[1] - 1 + 127, 0) - down, 1)
    scale = np.exp2(byte - 127.0)
    codes = (blocks / scale).astype(np.float32).astype(dtype).astype(np.float64)
    return np.moveaxis((codes * scale).reshape(v.shape), -1, axis)


WIDE = False


def mx_kscale(k):
    if not WIDE:
        return np.ones(k)
    levels = np.array([10, -10, 5, -5, 0])
    if k % 512:
        return np.exp2(np.random.permutation(np.resize(levels, k // 32))).repeat(32)
    a = np.empty((k // 512, 16))
    for p in range(k // 512):
        a[p, :8] = np.random.permutation(np.resize(levels, 8))
        for g in range(8):
            far = levels[np.abs(levels - a[p, g]) >= 10]
            a[p, g + 8] = far[np.random.randint(len(far))]
    return np.exp2(a.ravel()).repeat(32)


def f64(x):
    return np.asarray(x).astype(np.float64)


def striped(idx):
    return np.tile(idx.reshape(-1, 16).T, (8, 1)).astype(np.uint16)


def unstriped(offs):
    return offs[:16].T.reshape(-1).astype(np.int64)


def striped8(idx):
    return np.concatenate([x.reshape(-1, 16).T for x in idx]).astype(np.uint16)


def runs(offs, k):
    lists = np.stack([offs[16 * r : 16 * r + 16].T.reshape(-1) for r in range(8)]).astype(np.int64)
    return lists[np.arange(k) % 512 // 64]


def pack_weight(w):
    k, n = w.shape
    w = f64(np.asarray(w, np.float32).astype(ml_dtypes.bfloat16)).reshape(k // 32, 32, n)
    amax = np.abs(w).max(1)
    byte = np.clip(np.where(amax > 0, np.frexp(amax)[1] - 1 + 127 - 7, 1), 1, 254)
    scaled = (w * np.exp2(127.0 - byte)[:, None, :]).reshape(k, n).astype(np.float32)
    words = np.ascontiguousarray(scaled.reshape(k // 512, 128, 4, n).transpose(0, 1, 3, 2)).astype(ml_dtypes.float8_e4m3fn).view(np.uint8)
    return words, np.ascontiguousarray(byte.astype(np.uint8).reshape(k // 512, 16, n))


def unpack_weight(words, scales):
    g, p, n, _ = words.shape
    vals = np.ascontiguousarray(words).view(ml_dtypes.float8_e4m3fn).astype(np.float64) * np.repeat(np.exp2(scales.astype(np.float64) - 127.0), 8, axis=1)[..., None]
    return vals.transpose(0, 1, 3, 2).reshape(g * 512, n)


E2M1 = np.array([0.0, 0.5, 1.0, 1.5, 2.0, 3.0, 4.0, 6.0, -0.0, -0.5, -1.0, -1.5, -2.0, -3.0, -4.0, -6.0])


def pack_fp4(w):
    k, n = w.shape
    w = f64(np.asarray(w, np.float32).astype(ml_dtypes.bfloat16)).reshape(k // 32, 32, n)
    amax = np.abs(w).max(1)
    mant, ex = np.frexp(amax / 6.0)
    byte = np.clip(np.where(amax > 0, np.where(mant > 0.5, ex, ex - 1) + 127, 1), 1, 254)
    scaled = (w * np.exp2(127.0 - byte)[:, None, :]).reshape(k, n).astype(np.float32)
    c = np.ascontiguousarray(scaled.reshape(k // 512, 128, 4, n).transpose(0, 1, 3, 2)).astype(ml_dtypes.float4_e2m1fn).view(np.uint8) & 0xF
    words = (c[..., 0::2] | (c[..., 1::2] << 4)).reshape(k // 512, 128, 2 * n)
    return np.ascontiguousarray(words), np.ascontiguousarray(byte.astype(np.uint8).reshape(k // 512, 16, n))


def unpack_fp4(words, scales):
    g, _, n = scales.shape
    words = np.ascontiguousarray(words).reshape(g, 128, n, 2)
    nib = np.empty((g, 128, n, 4), np.uint8)
    nib[..., 0::2] = words & 0xF
    nib[..., 1::2] = words >> 4
    vals = E2M1[nib] * np.repeat(np.exp2(scales.astype(np.float64) - 127.0), 8, axis=1)[..., None]
    return vals.transpose(0, 1, 3, 2).reshape(g * 512, n)


def sigmoid(v):
    return 1.0 / (1.0 + np.exp(-np.maximum(v, -700.0)))

def planes(y):
    n, m = y.shape
    v = y.astype(np.float32).astype(ml_dtypes.bfloat16).astype(np.float64).reshape(n // 32, 32, m)
    top = np.abs(v).max(1)
    byte = np.clip(np.where(top > 0, np.frexp(top)[1] - 1 + 127 - 7, 1), 1, 254)
    codes = (v * np.exp2(127.0 - byte)[:, None, :]).reshape(n, m).astype(np.float32).astype(ml_dtypes.float8_e4m3fn).view(np.uint8)
    words = codes.reshape(n // 512, 128, 4, m).transpose(0, 1, 3, 2)
    return np.ascontiguousarray(words), np.ascontiguousarray(byte.astype(np.uint8).reshape(n // 512, 16, m))


K, T, S, V, G, H = 512, 1024, 512, 512, 2048, 512


def setup_inputs():
    n = np.random.standard_normal
    s = mx_kscale(K)[:, None]
    u = mx_kscale(S)
    packed_xT = pack_weight(n((K, T)) * s)
    packed_dT = pack_weight(n((K, G)) / s)
    packed_w1 = pack_fp4(n((K, H)) / np.sqrt(K) / s)
    return {
        "x_words": packed_xT[0],
        "x_scales": packed_xT[1],
        "d_words": packed_dT[0],
        "d_scales": packed_dT[1],
        "w1_words": packed_w1[0],
        "w1_scales": packed_w1[1],
        "ga": (np.random.uniform(0.5, 1.5, (H, 1)) * u[:, None]).astype(np.float32),
        "gb": (np.random.uniform(0.5, 1.5, (H, 1)) / u[:, None]).astype(np.float32),
        "offs": striped(np.random.permutation(T)[:S]),
        "k1": striped8(np.random.randint(0, G, (8, H))),
        "two": striped(np.random.permutation(T)[:V]),
        "n1": striped8(np.stack([np.random.permutation(S) for _ in range(8)])),
        "n2": striped8(np.stack([np.random.permutation(S) for _ in range(8)])),
        "n3": striped8(np.stack([np.random.permutation(V) for _ in range(8)])),
        "n4": striped8(np.stack([np.random.permutation(V) for _ in range(8)])),
        "n5": striped8(np.stack([np.random.permutation(V) for _ in range(8)])),
        "n6": striped8(np.stack([np.random.permutation(V) for _ in range(8)])),
        "n7": striped8(np.stack([np.random.permutation(V) for _ in range(8)])),
    }


def reference(x_words, x_scales, d_words, d_scales, w1_words, w1_scales, ga, gb, offs, k1, two, n1, n2, n3, n4, n5, n6, n7):
    d_k1 = unpack_weight(d_words, d_scales)[np.arange(K)[:, None], runs(k1, K)]
    xq = unpack_weight(x_words, x_scales)[:, unstriped(offs)]
    a = 0.0625 * (d_k1.T @ xq)
    z = f64(ga) * (a[np.arange(H)[:, None], runs(n1, H)] - (a[np.arange(H)[:, None], runs(n2, H)]))
    x_two = unpack_weight(x_words, x_scales)[:, unstriped(two)]
    b = unpack_fp4(w1_words, w1_scales).T @ x_two
    pa = b[np.arange(H)[:, None], runs(n3, H)]
    z2 = f64(gb) * (pa + (sigmoid(b[np.arange(H)[:, None], runs(n4, H)])) * (b[np.arange(H)[:, None], runs(n5, H)] - pa))
    s = 0.0625 * ((mxq(z, 0, "e4m3").T @ mxq(z2, 0, "e4m3")))
    out_0 = np.maximum(s * (sigmoid(s[np.arange(S)[:, None], runs(n6, S)])), s[np.arange(S)[:, None], runs(n7, S)])
    return (out_0,) + planes(out_0)

@@ -1,0 +1,281 @@
+from contextlib import ExitStack
+
+import concourse.mybir as mybir
+from concourse.masks import make_identity
+
+F32 = mybir.dt.float32
+BF16 = mybir.dt.bfloat16
+I32 = mybir.dt.int32
+U32 = mybir.dt.uint32
+U16 = mybir.dt.uint16
+U8 = mybir.dt.uint8
+FP8X4 = mybir.dt.float8_e4m3fn_x4
+FP4X4 = mybir.dt.float4_e2m1fn_x4
+ACT = mybir.ActivationFunctionType
+ALU = mybir.AluOpType
+
+P = 128
+PACK = 4
+N = 512
+T = 1024
+G = 2048
+HALF = N // 2
+LANES = 16
+OUT_SLICES = ((0, 256), (256, 128), (384, 128))
+FLOPS = 3 * 2 * 512 * 512 * 512
+
+
+def entries(offsets, first, count):
+    return offsets[:, first // LANES : (first + count) // LANES]
+
+
+def deal(engine, dst, src, run):
+    engine.tensor_copy(
+        out=dst.rearrange("p (t b j) -> p t b j", t=PACK, j=run),
+        in_=src.rearrange("p (b t j) -> p t b j", t=PACK, j=run),
+    )
+
+
+def tile_picked_ckqgaplerpgmax_none_po_kernel(
+    tc, x_words, x_scales, d_words, d_scales, w1_words, w1_scales, ga, gb,
+    offs, k1, two, n1, n2, n3, n4, n5, n6, n7, out_0, out_1, out_2,
+):
+    nc = tc.nc
+    with ExitStack() as ctx:
+        lists = ctx.enter_context(tc.tile_pool(name="lists", bufs=1))
+        keep = ctx.enter_context(tc.tile_pool(name="keep", bufs=1))
+        psum = ctx.enter_context(tc.psum_pool(name="psum", bufs=1))
+
+        def sb(name, shape, dtype):
+            return keep.tile(shape, dtype, name=name, align_bytes=64)
+
+        def bank(i, name):
+            return psum.tile([P, N], F32, name=name, tag="bank%d" % i)
+
+        def load_list(name, src):
+            tile = lists.tile([P, N // LANES], U16, name=name)
+            nc.sync.dma_start(tile[:], src)
+            return tile
+
+        def load_scale_rows(queue, plane, rows):
+            for q in range(4):
+                queue.dma_start(plane[32 * q : 32 * q + 4, :].bitcast(I32), rows[4 * q : 4 * q + 4, :].bitcast(I32))
+
+        xs_table = sb("xs_table", [P, T], U8)
+        ds_table = sb("ds_table", [P, G], U8)
+        w1s_raw = sb("w1s_raw", [P, N], U8)
+        ds_plane = sb("ds_plane", [P, N], U8)
+        gain_rows = sb("gain_rows", [P, P], F32)
+        ident = sb("ident", [P, P], F32)
+        warm = sb("warm", [P, 2], F32)
+        nc.vector.memset(xs_table[:].bitcast(I32), 0)
+        nc.vector.memset(ds_table[:].bitcast(I32), 0)
+        nc.vector.memset(w1s_raw[:].bitcast(I32), 0)
+        nc.gpsimd.memset(warm[:], 0.0)
+        nc.scalar.activation(warm[:, 1:2], warm[:, 0:1], ACT.Sigmoid)
+        nc.gpsimd.memset(gain_rows[:], 0.0)
+        nc.gpsimd.dma_start(gain_rows[4:8, :].rearrange("t (b j) -> t b j", j=8), gb.rearrange("(b t j) o -> t b (j o)", t=PACK, j=8))
+        nc.gpsimd.dma_start(gain_rows[0:4, :].rearrange("t (b j) -> t b j", j=8), ga.rearrange("(b t j) o -> t b (j o)", t=PACK, j=8))
+        make_identity(nc, ident[:])
+        nc.gpsimd.memset(ds_plane[:].bitcast(I32), 0)
+
+        xw_table = sb("xw_table", [P, T], I32)
+        dw_table = sb("dw_table", [P, G], I32)
+        w1w_raw = sb("w1w_raw", [P, N // 2], I32)
+
+        two_t = load_list("two_t", two)
+        load_scale_rows(nc.sync, xs_table, x_scales[0])
+        k1_t = load_list("k1_t", k1)
+        nc.sync.dma_start(ds_table[0:P:8, :].bitcast(I32), d_scales[0].bitcast(I32))
+        nc.sync.dma_start(xw_table[:], x_words[0].rearrange("p n t -> p (n t)").bitcast(I32))
+        nc.sync.dma_start(w1w_raw[:], w1_words[0].bitcast(I32))
+        load_scale_rows(nc.sync, w1s_raw, w1_scales[0])
+        offs_t = load_list("offs_t", offs)
+        n4_t = load_list("n4_t", n4)
+        nc.sync.dma_start(dw_table[:], d_words[0].rearrange("p n t -> p (n t)").bitcast(I32))
+        n3_t = load_list("n3_t", n3)
+        n5_t = load_list("n5_t", n5)
+        n2_t = load_list("n2_t", n2)
+        n1_t = load_list("n1_t", n1)
+        n6_t = load_list("n6_t", n6)
+        n7_t = load_list("n7_t", n7)
+
+        gain_ps = bank(7, "gain_ps")
+        nc.tensor.transpose(gain_ps[:, 0:P], gain_rows[:], ident[:])
+        ga16 = sb("ga16", [P, PACK], F32)
+        gb_pos = sb("gb_pos", [P, PACK], F32)
+        gb_neg = sb("gb_neg", [P, PACK], F32)
+        nc.scalar.activation(gb_pos[:], gain_ps[:, 4:8], ACT.Copy)
+        nc.scalar.activation(gb_neg[:], gain_ps[:, 4:8], ACT.Copy, scale=-1.0)
+        nc.scalar.activation(ga16[:], gain_ps[:, 0:4], ACT.Copy, scale=0.0625)
+
+        def gather_words(name, table, offsets):
+            picked = sb(name, [P, N], I32)
+            nc.vector.tensor_copy(picked[:].bitcast(U32), table[:].bitcast(U32).indirect(offsets[:]))
+            return picked
+
+        def gather_bytes(name, table, offsets):
+            picked = sb(name, [P, N], U8)
+            nc.vector.tensor_copy(picked[:], table[:].indirect(offsets[:]))
+            return picked
+
+        two_s = gather_bytes("two_s", xs_table, two_t)
+        k1_s = gather_bytes("k1_s", ds_table, k1_t)
+        two_w = gather_words("two_w", xw_table, two_t)
+        w1w = sb("w1w", [P, N // 2], I32)
+        w1s = sb("w1s", [P, N], U8)
+        deal(nc.vector, w1w[:], w1w_raw[:], 4)
+        deal(nc.vector, w1s[:].bitcast(I32), w1s_raw[:].bitcast(I32), 2)
+
+        b_win = []
+        for t in range(PACK):
+            acc = bank(t, "b_ps%d" % t)
+            nc.tensor.matmul_mx(
+                out=acc[:],
+                lhsT=w1w[:].bitcast(U8)[:, 2 * P * t : 2 * P * (t + 1)].bitcast(FP4X4),
+                lhsT_scale=w1s[:, P * t : P * (t + 1)],
+                rhs=two_w[:].bitcast(FP8X4),
+                rhs_scale=two_s[:],
+                start=True, stop=True,
+            )
+            win = sb("b_win%d" % t, [P, N], F32)
+            nc.scalar.activation(win[:], acc[:], ACT.Copy)
+            b_win.append(win)
+
+        k1_sd = sb("k1_sd", [P, N], U8)
+        deal(nc.vector, k1_sd[:].bitcast(I32), k1_s[:].bitcast(I32), 2)
+        for q in range(4):
+            nc.sync.dma_start(ds_plane[32 * q : 32 * q + 4, :].bitcast(I32), k1_sd[32 * q : 32 * q + 32 : 8, :].bitcast(I32))
+        offs_s = gather_bytes("offs_s", xs_table, offs_t)
+        offs_w = gather_words("offs_w", xw_table, offs_t)
+        k1_w = gather_words("k1_w", dw_table, k1_t)
+        k1_wd = sb("k1_wd", [P, N], I32)
+        deal(nc.vector, k1_wd[:], k1_w[:], 8)
+
+        z2_bf = sb("z2_bf", [P, N, PACK], BF16)
+        z2_codes = sb("z2_codes", [P, N], I32)
+        z2_plane = sb("z2_plane", [P, N], U8)
+        z_bf = sb("z_bf", [P, PACK, P, PACK], BF16)
+        z_codes = sb("z_codes", [P, N], I32)
+        z_plane = sb("z_plane", [P, N], U8)
+
+        def b_half(h):
+            first = h * HALF
+            keep_part = sb("keep_part%d" % h, [P, PACK, HALF], F32)
+            take_part = sb("take_part%d" % h, [P, PACK, HALF], F32)
+            for t in range(PACK):
+                gate = sb("gate%d_%d" % (h, t), [P, HALF], F32)
+                take = sb("take%d_%d" % (h, t), [P, HALF], F32)
+                rest = sb("rest%d_%d" % (h, t), [P, HALF], F32)
+                nc.scalar.activation(gate[:], b_win[t][:].indirect(entries(n4_t, first, HALF)), ACT.Sigmoid)
+                nc.scalar.activation(rest[:], gate[:], ACT.Identity, scale=gb_neg[:, t : t + 1], bias=gb_pos[:, t : t + 1])
+                nc.scalar.activation(take[:], gate[:], ACT.Copy, scale=gb_pos[:, t : t + 1])
+                nc.vector.tensor_tensor(keep_part[:, t, :], b_win[t][:].indirect(entries(n3_t, first, HALF)), rest[:], ALU.mult)
+                nc.vector.tensor_tensor(take_part[:, t, :], b_win[t][:].indirect(entries(n5_t, first, HALF)), take[:], ALU.mult)
+            nc.vector.tensor_tensor(
+                z2_bf[:, first : first + HALF, :].rearrange("p (c i) t -> p c t i", i=4),
+                keep_part[:].rearrange("p t (c i) -> p c t i", i=4),
+                take_part[:].rearrange("p t (c i) -> p c t i", i=4),
+                ALU.add,
+            )
+            nc.vector.quantize_mx(
+                out=z2_codes[:, first : first + HALF].bitcast(FP8X4),
+                scales=z2_plane[:, first : first + HALF],
+                in_=z2_bf[:, first : first + HALF, :].rearrange("p v t -> p (v t)"),
+            )
+
+        a_win = []
+
+        def a_products():
+            for t in range(PACK):
+                acc = bank(PACK + t, "a_ps%d" % t)
+                nc.tensor.matmul_mx(
+                    out=acc[:],
+                    lhsT=k1_wd[:, P * t : P * (t + 1)].bitcast(FP8X4),
+                    lhsT_scale=ds_plane[:, P * t : P * (t + 1)],
+                    rhs=offs_w[:].bitcast(FP8X4),
+                    rhs_scale=offs_s[:],
+                    start=True, stop=True,
+                )
+                win = sb("a_win%d" % t, [P, N], F32)
+                nc.scalar.activation(win[:], acc[:], ACT.Copy, scale=ga16[:, t : t + 1])
+                a_win.append(win)
+
+        def a_slice(first, count, on_vector):
+            diff = sb("diff%d" % first, [P, PACK, count], F32)
+            minus = sb("minus%d" % first, [P, PACK, count], F32)
+            for t in range(PACK):
+                nc.vector.tensor_copy(minus[:, t, :], a_win[t][:].indirect(entries(n2_t, first, count)))
+            for t in range(PACK):
+                nc.vector.tensor_tensor(diff[:, t, :], a_win[t][:].indirect(entries(n1_t, first, count)), minus[:, t, :], ALU.subtract)
+            dst = z_bf[:, :, first // PACK : (first + count) // PACK, :].rearrange("p c m t -> p m t c")
+            src = diff[:].rearrange("p t (m c) -> p m t c", c=PACK)
+            if on_vector:
+                nc.vector.tensor_copy(dst, src)
+            else:
+                nc.scalar.copy(dst, src)
+
+        b_half(0)
+        a_products()
+        a_slice(0, 256, False)
+        b_half(1)
+        a_slice(256, 128, False)
+        a_slice(384, 128, True)
+
+        s_win = []
+        for c in range(PACK):
+            cols = slice(P * c, P * (c + 1))
+            nc.vector.quantize_mx(
+                out=z_codes[:, cols].bitcast(FP8X4),
+                scales=z_plane[:, cols],
+                in_=z_bf[:, c, :, :].rearrange("p m t -> p (m t)"),
+            )
+            acc = bank(c, "s_ps%d" % c)
+            nc.tensor.matmul_mx(
+                out=acc[:],
+                lhsT=z_codes[:, cols].bitcast(FP8X4),
+                lhsT_scale=z_plane[:, cols],
+                rhs=z2_codes[:].bitcast(FP8X4),
+                rhs_scale=z2_plane[:],
+                start=True, stop=True,
+            )
+            win = sb("s_win%d" % c, [P, N], F32)
+            if c == 0:
+                nc.vector.tensor_scalar(win[:], acc[:], 0.0625, None, ALU.mult)
+            else:
+                nc.scalar.activation(win[:], acc[:], ACT.Copy, scale=0.0625)
+            s_win.append(win)
+
+        y_bf = sb("y_bf", [P, N, PACK], BF16)
+        y_codes = sb("y_codes", [P, N], I32)
+        y_plane = sb("y_plane", [P, N], U8)
+        out_rows = out_0.rearrange("(m c) v -> m c v", c=PACK)
+        out_words = out_1[0].rearrange("p n t -> p (n t)").bitcast(I32)
+        for first, count in OUT_SLICES:
+            cols = slice(first, first + count)
+            gate6 = sb("gate6_%d" % first, [P, PACK, count], F32)
+            other = sb("other%d" % first, [P, PACK, count], F32)
+            gated = sb("gated%d" % first, [P, PACK, count], F32)
+            y = sb("y%d" % first, [P, PACK, count], F32)
+            for c in range(PACK):
+                nc.scalar.activation(gate6[:, c, :], s_win[c][:].indirect(entries(n6_t, first, count)), ACT.Sigmoid)
+                nc.vector.tensor_copy(other[:, c, :], s_win[c][:].indirect(entries(n7_t, first, count)))
+            for c in range(PACK):
+                nc.vector.tensor_tensor(gated[:, c, :], s_win[c][:, cols], gate6[:, c, :], ALU.mult)
+            nc.vector.tensor_tensor(y[:], gated[:], other[:], ALU.max)
+            nc.sync.dma_start(out_rows[:, :, cols], y[:])
+            dst = y_bf[:, cols, :].rearrange("p (c i) t -> p c t i", i=4)
+            src = y[:].rearrange("p t (c i) -> p c t i", i=4)
+            if first + count == N:
+                nc.vector.tensor_copy(dst, src)
+            else:
+                nc.scalar.copy(dst, src)
+            nc.vector.quantize_mx(
+                out=y_codes[:, cols].bitcast(FP8X4),
+                scales=y_plane[:, cols],
+                in_=y_bf[:, cols, :].rearrange("p v t -> p (v t)"),
+            )
+            nc.sync.dma_start(out_words[:, cols], y_codes[:, cols])
+        for q in range(4):
+            queue = nc.sync if q % 2 == 0 else nc.scalar
+            queue.dma_start(out_2[0][4 * q : 4 * q + 4, :].bitcast(I32), y_plane[32 * q : 32 * q + 4, :].bitcast(I32))

@@ -68,16 +68,17 @@ def tile_picked_ckqgaplerpgmax_none_po_kernel(
         gain_rows = sb("gain_rows", [P, P], F32)
         ident = sb("ident", [P, P], F32)
         warm = sb("warm", [P, 2], F32)
-        nc.vector.memset(xs_table[:].bitcast(I32), 0)
-        nc.vector.memset(ds_table[:].bitcast(I32), 0)
-        nc.vector.memset(w1s_raw[:].bitcast(I32), 0)
+        nc.gpsimd.memset(xs_table[:].bitcast(I32), 0)
         nc.gpsimd.memset(warm[:], 0.0)
         nc.scalar.activation(warm[:, 1:2], warm[:, 0:1], ACT.Sigmoid)
-        nc.gpsimd.memset(gain_rows[:], 0.0)
+        nc.vector.memset(gain_rows[:], 0.0)
+        nc.vector.memset(ds_table[:].bitcast(I32), 0)
+        nc.vector.memset(ident[:], 0.0)
+        nc.vector.memset(w1s_raw[:].bitcast(I32), 0)
+        nc.vector.memset(ds_plane[:].bitcast(I32), 0)
         nc.gpsimd.dma_start(gain_rows[4:8, :].rearrange("t (b j) -> t b j", j=8), gb.rearrange("(b t j) o -> t b (j o)", t=PACK, j=8))
         nc.gpsimd.dma_start(gain_rows[0:4, :].rearrange("t (b j) -> t b j", j=8), ga.rearrange("(b t j) o -> t b (j o)", t=PACK, j=8))
-        make_identity(nc, ident[:])
-        nc.gpsimd.memset(ds_plane[:].bitcast(I32), 0)
+        make_identity(nc, ident[:], nomemset=True)
 
         xw_table = sb("xw_table", [P, T], I32)
         dw_table = sb("dw_table", [P, G], I32)
@@ -95,19 +96,6 @@ def tile_picked_ckqgaplerpgmax_none_po_kernel(
         nc.sync.dma_start(dw_table[:], d_words[0].rearrange("p n t -> p (n t)").bitcast(I32))
         n3_t = load_list("n3_t", n3)
         n5_t = load_list("n5_t", n5)
-        n2_t = load_list("n2_t", n2)
-        n1_t = load_list("n1_t", n1)
-        n6_t = load_list("n6_t", n6)
-        n7_t = load_list("n7_t", n7)
-
-        gain_ps = bank(7, "gain_ps")
-        nc.tensor.transpose(gain_ps[:, 0:P], gain_rows[:], ident[:])
-        ga16 = sb("ga16", [P, PACK], F32)
-        gb_pos = sb("gb_pos", [P, PACK], F32)
-        gb_neg = sb("gb_neg", [P, PACK], F32)
-        nc.scalar.activation(gb_pos[:], gain_ps[:, 4:8], ACT.Copy)
-        nc.scalar.activation(gb_neg[:], gain_ps[:, 4:8], ACT.Copy, scale=-1.0)
-        nc.scalar.activation(ga16[:], gain_ps[:, 0:4], ACT.Copy, scale=0.0625)
 
         def gather_words(name, table, offsets):
             picked = sb(name, [P, N], I32)
@@ -122,12 +110,20 @@ def tile_picked_ckqgaplerpgmax_none_po_kernel(
         two_s = gather_bytes("two_s", xs_table, two_t)
         k1_s = gather_bytes("k1_s", ds_table, k1_t)
         two_w = gather_words("two_w", xw_table, two_t)
+        k1_sd = sb("k1_sd", [P, N], U8)
+        deal(nc.vector, k1_sd[:].bitcast(I32), k1_s[:].bitcast(I32), 2)
+        for q in range(4):
+            nc.sync.dma_start(ds_plane[32 * q : 32 * q + 4, :].bitcast(I32), k1_sd[32 * q : 32 * q + 32 : 8, :].bitcast(I32))
+        n2_t = load_list("n2_t", n2)
+        n1_t = load_list("n1_t", n1)
+        n6_t = load_list("n6_t", n6)
+        n7_t = load_list("n7_t", n7)
         w1w = sb("w1w", [P, N // 2], I32)
         w1s = sb("w1s", [P, N], U8)
         deal(nc.vector, w1w[:], w1w_raw[:], 4)
         deal(nc.vector, w1s[:].bitcast(I32), w1s_raw[:].bitcast(I32), 2)
 
-        b_win = []
+        b_acc = []
         for t in range(PACK):
             acc = bank(t, "b_ps%d" % t)
             nc.tensor.matmul_mx(
@@ -138,144 +134,240 @@ def tile_picked_ckqgaplerpgmax_none_po_kernel(
                 rhs_scale=two_s[:],
                 start=True, stop=True,
             )
-            win = sb("b_win%d" % t, [P, N], F32)
-            nc.scalar.activation(win[:], acc[:], ACT.Copy)
-            b_win.append(win)
+            b_acc.append(acc)
+        b_win = [sb("b_win%d" % t, [P, N], F32) for t in range(PACK)]
 
-        k1_sd = sb("k1_sd", [P, N], U8)
-        deal(nc.vector, k1_sd[:].bitcast(I32), k1_s[:].bitcast(I32), 2)
-        for q in range(4):
-            nc.sync.dma_start(ds_plane[32 * q : 32 * q + 4, :].bitcast(I32), k1_sd[32 * q : 32 * q + 32 : 8, :].bitcast(I32))
+        gain_ps = bank(7, "gain_ps")
+        nc.tensor.transpose(gain_ps[:, 0:P], gain_rows[:], ident[:])
+        ga16 = keep.tile([P, PACK], F32, name="ga16", tag="terms2", align_bytes=64)
+        gb_pos = sb("gb_pos", [P, PACK], F32)
+        gb_neg = sb("gb_neg", [P, PACK], F32)
+        nc.scalar.activation(gb_pos[:], gain_ps[:, 4:8], ACT.Copy)
+        nc.scalar.activation(gb_neg[:], gain_ps[:, 4:8], ACT.Copy, scale=-1.0)
+        nc.scalar.activation(ga16[:], gain_ps[:, 0:4], ACT.Copy, scale=0.0625)
+
+
         offs_s = gather_bytes("offs_s", xs_table, offs_t)
         offs_w = gather_words("offs_w", xw_table, offs_t)
         k1_w = gather_words("k1_w", dw_table, k1_t)
         k1_wd = sb("k1_wd", [P, N], I32)
         deal(nc.vector, k1_wd[:], k1_w[:], 8)
 
-        z2_bf = sb("z2_bf", [P, N, PACK], BF16)
+        z2_bf = sb("z2_bf", [P, N * PACK], BF16)
         z2_codes = sb("z2_codes", [P, N], I32)
         z2_plane = sb("z2_plane", [P, N], U8)
-        z_bf = sb("z_bf", [P, PACK, P, PACK], BF16)
+        z_bf = sb("z_bf", [P, N * PACK], BF16)
         z_codes = sb("z_codes", [P, N], I32)
         z_plane = sb("z_plane", [P, N], U8)
 
-        def b_half(h):
-            first = h * HALF
-            keep_part = sb("keep_part%d" % h, [P, PACK, HALF], F32)
-            take_part = sb("take_part%d" % h, [P, PACK, HALF], F32)
+        def b_take(first, t, gate, tag):
+            take = keep.tile([P, HALF], F32, name="take%d_%d" % (first, t), tag=tag, align_bytes=64)
+            nc.scalar.activation(take[:], gate[:], ACT.Copy, scale=gb_pos[:, t : t + 1])
+            return take
+
+        def b_gates(first, count):
+            made = []
             for t in range(PACK):
-                gate = sb("gate%d_%d" % (h, t), [P, HALF], F32)
-                take = sb("take%d_%d" % (h, t), [P, HALF], F32)
-                rest = sb("rest%d_%d" % (h, t), [P, HALF], F32)
-                nc.scalar.activation(gate[:], b_win[t][:].indirect(entries(n4_t, first, HALF)), ACT.Sigmoid)
+                if first == 0:
+                    nc.scalar.activation(b_win[t][:], b_acc[t][:], ACT.Copy)
+                gate = sb("gate%d_%d" % (first, t), [P, count], F32)
+                rest = sb("rest%d_%d" % (first, t), [P, count], F32)
+                nc.scalar.activation(gate[:], b_win[t][:].indirect(entries(n4_t, first, count)), ACT.Sigmoid)
                 nc.scalar.activation(rest[:], gate[:], ACT.Identity, scale=gb_neg[:, t : t + 1], bias=gb_pos[:, t : t + 1])
-                nc.scalar.activation(take[:], gate[:], ACT.Copy, scale=gb_pos[:, t : t + 1])
-                nc.vector.tensor_tensor(keep_part[:, t, :], b_win[t][:].indirect(entries(n3_t, first, HALF)), rest[:], ALU.mult)
-                nc.vector.tensor_tensor(take_part[:, t, :], b_win[t][:].indirect(entries(n5_t, first, HALF)), take[:], ALU.mult)
-            nc.vector.tensor_tensor(
-                z2_bf[:, first : first + HALF, :].rearrange("p (c i) t -> p c t i", i=4),
-                keep_part[:].rearrange("p t (c i) -> p c t i", i=4),
-                take_part[:].rearrange("p t (c i) -> p c t i", i=4),
-                ALU.add,
-            )
-            nc.vector.quantize_mx(
-                out=z2_codes[:, first : first + HALF].bitcast(FP8X4),
-                scales=z2_plane[:, first : first + HALF],
-                in_=z2_bf[:, first : first + HALF, :].rearrange("p v t -> p (v t)"),
-            )
+                if first == HALF and t == PACK - 1:
+                    made.append((rest, gate))
+                    continue
+                made.append((rest, b_take(first, t, gate, "take%d_%d" % (first, t))))
+            return made
 
-        a_win = []
+        def terms(tag, name, count):
+            both = keep.tile([P, 2, PACK, count], F32, name="terms_" + name, tag="terms" + tag, align_bytes=64)
+            return both[:, 0, :, :], both[:, 1, :, :]
 
-        def a_products():
+        def b_terms(tag, first, count, gates):
+            left, right = terms(tag, "b%d" % first, count)
+            for t, (rest, take) in enumerate(gates):
+                nc.vector.tensor_tensor(left[:, t, :], b_win[t][:].indirect(entries(n3_t, first, count)), rest[:], ALU.mult)
+                if first == HALF and t == PACK - 1:
+                    take = b_take(first, t, take, "rounded_a%d_1" % HALF)
+                    quantize_z()
+                nc.vector.tensor_tensor(right[:, t, :], b_win[t][:].indirect(entries(n5_t, first, count)), take[:], ALU.mult)
+            return left, right
+
+        def a_terms(tag, first, count):
+            left, right = terms(tag, "a%d" % first, count)
             for t in range(PACK):
-                acc = bank(PACK + t, "a_ps%d" % t)
-                nc.tensor.matmul_mx(
-                    out=acc[:],
-                    lhsT=k1_wd[:, P * t : P * (t + 1)].bitcast(FP8X4),
-                    lhsT_scale=ds_plane[:, P * t : P * (t + 1)],
-                    rhs=offs_w[:].bitcast(FP8X4),
-                    rhs_scale=offs_s[:],
-                    start=True, stop=True,
+                nc.vector.tensor_copy(left[:, t, :], a_win[t][:].indirect(entries(n1_t, first, count)))
+                nc.vector.tensor_scalar(right[:, t, :], a_win[t][:].indirect(entries(n2_t, first, count)), -1.0, 0.0, ALU.mult, ALU.add)
+            return left, right
+
+        def add_and_round(name, left, right, count, bank0):
+            chunks = count // P
+            back = bank(2 + turn[0] % 2, "back_" + name)
+            turn[0] = turn[0] + 1
+            for k in range(chunks):
+                cols = slice(P * k, P * (k + 1))
+                summed = bank(bank0 + k, "sum_%s_%d" % (name, k))
+                for t in range(PACK):
+                    dst = summed[:, P * t : P * (t + 1)]
+                    nc.tensor.matmul(dst, left[:, t, cols], ident[:], start=True, stop=False, is_transpose=True)
+                    nc.tensor.matmul(dst, right[:, t, cols], ident[:], start=False, stop=True, is_transpose=True)
+                rounded = keep.tile([P, N], BF16, name="rounded", tag="rounded_%s_%d" % (name, k), align_bytes=64)
+                nc.scalar.copy(
+                    rounded[:].rearrange("v (u p e) -> v u p e", u=2, e=2),
+                    summed[:].rearrange("v (u e p) -> v u p e", u=2, e=2),
                 )
-                win = sb("a_win%d" % t, [P, N], F32)
-                nc.scalar.activation(win[:], acc[:], ACT.Copy, scale=ga16[:, t : t + 1])
-                a_win.append(win)
+                for u in range(2):
+                    nc.tensor.transpose(
+                        back[:, P * (2 * k + u) : P * (2 * k + u + 1)],
+                        rounded[:].bitcast(F32)[:, P * u : P * (u + 1)],
+                        ident[:],
+                    )
+            return back[:, 0 : 2 * count].rearrange("p (k u v) -> p k u v", u=2, v=P)
 
-        def a_slice(first, count, on_vector):
-            diff = sb("diff%d" % first, [P, PACK, count], F32)
-            minus = sb("minus%d" % first, [P, PACK, count], F32)
-            for t in range(PACK):
-                nc.vector.tensor_copy(minus[:, t, :], a_win[t][:].indirect(entries(n2_t, first, count)))
-            for t in range(PACK):
-                nc.vector.tensor_tensor(diff[:, t, :], a_win[t][:].indirect(entries(n1_t, first, count)), minus[:, t, :], ALU.subtract)
-            dst = z_bf[:, :, first // PACK : (first + count) // PACK, :].rearrange("p c m t -> p m t c")
-            src = diff[:].rearrange("p t (m c) -> p m t c", c=PACK)
-            if on_vector:
-                nc.vector.tensor_copy(dst, src)
-            else:
-                nc.scalar.copy(dst, src)
-
-        b_half(0)
-        a_products()
-        a_slice(0, 256, False)
-        b_half(1)
-        a_slice(256, 128, False)
-        a_slice(384, 128, True)
-
-        s_win = []
-        for c in range(PACK):
-            cols = slice(P * c, P * (c + 1))
+        def quantize_z2(first, count):
             nc.vector.quantize_mx(
-                out=z_codes[:, cols].bitcast(FP8X4),
-                scales=z_plane[:, cols],
-                in_=z_bf[:, c, :, :].rearrange("p m t -> p (m t)"),
+                out=z2_codes[:, first : first + count].bitcast(FP8X4),
+                scales=z2_plane[:, first : first + count],
+                in_=z2_bf[:, PACK * first : PACK * (first + count)],
             )
-            acc = bank(c, "s_ps%d" % c)
+
+        def b_finish(first, count, left, right):
+            back = add_and_round("b%d" % first, left, right, count, 0)
+            words = z2_bf[:].bitcast(F32)[:, 2 * first : 2 * (first + count)]
+            nc.scalar.copy(words.rearrange("p (k v u) -> p k v u", u=2, v=P), back.rearrange("p k u v -> p k v u"))
+            quantize_z2(first, count)
+
+        def a_finish(first, count, left, right):
+            back = add_and_round("a%d" % first, left, right, count, 4 if first == 0 else 0)
+            words = z_bf[:].bitcast(F32).rearrange("p (c m u) -> p m c u", c=PACK, u=2)
+            per = P // PACK
+            for k in range(count // P):
+                m0 = first // PACK + per * k
+                nc.scalar.copy(words[:, m0 : m0 + per, :, :], back[:, k, :, :].rearrange("p u (m c) -> p m c u", c=PACK))
+
+        def quantize_z():
+            for c in range(PACK):
+                nc.vector.quantize_mx(
+                    out=z_codes[:, P * c : P * (c + 1)].bitcast(FP8X4),
+                    scales=z_plane[:, P * c : P * (c + 1)],
+                    in_=z_bf[:, N * c : N * (c + 1)],
+                )
+
+        turn = [0]
+        gates0 = b_gates(0, HALF)
+        b0 = b_terms("0", 0, HALF, gates0)
+        a_win = []
+        for t in range(PACK):
+            acc = bank(PACK + t, "a_ps%d" % t)
             nc.tensor.matmul_mx(
                 out=acc[:],
-                lhsT=z_codes[:, cols].bitcast(FP8X4),
-                lhsT_scale=z_plane[:, cols],
-                rhs=z2_codes[:].bitcast(FP8X4),
-                rhs_scale=z2_plane[:],
+                lhsT=k1_wd[:, P * t : P * (t + 1)].bitcast(FP8X4),
+                lhsT_scale=ds_plane[:, P * t : P * (t + 1)],
+                rhs=offs_w[:].bitcast(FP8X4),
+                rhs_scale=offs_s[:],
                 start=True, stop=True,
             )
-            win = sb("s_win%d" % c, [P, N], F32)
+            win = sb("a_win%d" % t, [P, N], F32)
+            nc.scalar.activation(win[:], acc[:], ACT.Copy, scale=ga16[:, t : t + 1])
+            a_win.append(win)
+        gates1 = b_gates(HALF, HALF)
+        a0 = a_terms("1", 0, HALF)
+        b_finish(0, HALF, *b0)
+        a1 = a_terms("2", HALF, HALF)
+        a_finish(0, HALF, *a0)
+        a_finish(HALF, HALF, *a1)
+        b1 = b_terms("1", HALF, HALF, gates1)
+
+        s_acc = [bank(PACK + c, "s_ps%d" % c) for c in range(PACK)]
+        s_win = [sb("s_win%d" % c, [P, N], F32) for c in range(PACK)]
+
+        def s_product(c, first, count):
+            rows = slice(P * c, P * (c + 1))
+            cols = slice(first, first + count)
+            nc.tensor.matmul_mx(
+                out=s_acc[c][:, cols],
+                lhsT=z_codes[:, rows].bitcast(FP8X4),
+                lhsT_scale=z_plane[:, rows],
+                rhs=z2_codes[:, cols].bitcast(FP8X4),
+                rhs_scale=z2_plane[:, cols],
+                start=True, stop=True,
+            )
+
+        for c in range(PACK):
+            s_product(c, 0, HALF)
+            nc.scalar.activation(s_win[c][:, 0:HALF], s_acc[c][:, 0:HALF], ACT.Copy, scale=0.0625)
+        for k in range(2):
+            first = HALF + P * k
+            nc.vector.tensor_tensor(
+                z2_bf[:, PACK * first : PACK * (first + P)].rearrange("p (c i t) -> p c t i", i=4, t=PACK),
+                b1[0][:, :, P * k : P * (k + 1)].rearrange("p t (c i) -> p c t i", i=4),
+                b1[1][:, :, P * k : P * (k + 1)].rearrange("p t (c i) -> p c t i", i=4),
+                ALU.add,
+            )
+        quantize_z2(256, P)
+        quantize_z2(384, P)
+        for c in range(PACK):
+            s_product(c, 256, P)
+            s_product(c, 384, P)
             if c == 0:
-                nc.vector.tensor_scalar(win[:], acc[:], 0.0625, None, ALU.mult)
+                nc.vector.tensor_scalar(s_win[c][:, HALF:], s_acc[c][:, HALF:], 0.0625, None, ALU.mult)
             else:
-                nc.scalar.activation(win[:], acc[:], ACT.Copy, scale=0.0625)
-            s_win.append(win)
+                nc.scalar.activation(s_win[c][:, HALF:], s_acc[c][:, HALF:], ACT.Copy, scale=0.0625)
 
         y_bf = sb("y_bf", [P, N, PACK], BF16)
         y_codes = sb("y_codes", [P, N], I32)
         y_plane = sb("y_plane", [P, N], U8)
         out_rows = out_0.rearrange("(m c) v -> m c v", c=PACK)
         out_words = out_1[0].rearrange("p n t -> p (n t)").bitcast(I32)
-        for first, count in OUT_SLICES:
-            cols = slice(first, first + count)
-            gate6 = sb("gate6_%d" % first, [P, PACK, count], F32)
-            other = sb("other%d" % first, [P, PACK, count], F32)
-            gated = sb("gated%d" % first, [P, PACK, count], F32)
-            y = sb("y%d" % first, [P, PACK, count], F32)
+
+        def out_terms(first):
+            cols = slice(first, first + HALF)
+            gate6 = sb("gate6_%d" % first, [P, PACK, HALF], F32)
+            other = sb("other%d" % first, [P, PACK, HALF], F32)
+            gated = sb("gated%d" % first, [P, PACK, HALF], F32)
             for c in range(PACK):
-                nc.scalar.activation(gate6[:, c, :], s_win[c][:].indirect(entries(n6_t, first, count)), ACT.Sigmoid)
-                nc.vector.tensor_copy(other[:, c, :], s_win[c][:].indirect(entries(n7_t, first, count)))
+                nc.scalar.activation(gate6[:, c, :], s_win[c][:].indirect(entries(n6_t, first, HALF)), ACT.Sigmoid)
+                nc.vector.tensor_copy(other[:, c, :], s_win[c][:].indirect(entries(n7_t, first, HALF)))
             for c in range(PACK):
                 nc.vector.tensor_tensor(gated[:, c, :], s_win[c][:, cols], gate6[:, c, :], ALU.mult)
-            nc.vector.tensor_tensor(y[:], gated[:], other[:], ALU.max)
-            nc.sync.dma_start(out_rows[:, :, cols], y[:])
-            dst = y_bf[:, cols, :].rearrange("p (c i) t -> p c t i", i=4)
+            return gated, other
+
+        def out_max(first, count, gated, other):
+            part = slice(first % HALF, first % HALF + count)
+            y = sb("y%d" % first, [P, PACK, count], F32)
+            nc.vector.tensor_tensor(y[:], gated[:, :, part], other[:, :, part], ALU.max)
+            nc.sync.dma_start(out_rows[:, :, first : first + count], y[:])
+            return y
+
+        def out_round(first, count, y):
+            dst = y_bf[:, first : first + count, :].rearrange("p (c i) t -> p c t i", i=4)
             src = y[:].rearrange("p t (c i) -> p c t i", i=4)
             if first + count == N:
                 nc.vector.tensor_copy(dst, src)
             else:
                 nc.scalar.copy(dst, src)
+
+        def out_planes(first, count):
+            cols = slice(first, first + count)
             nc.vector.quantize_mx(
                 out=y_codes[:, cols].bitcast(FP8X4),
                 scales=y_plane[:, cols],
                 in_=y_bf[:, cols, :].rearrange("p v t -> p (v t)"),
             )
             nc.sync.dma_start(out_words[:, cols], y_codes[:, cols])
+
+        terms0 = out_terms(0)
+        terms1 = out_terms(HALF)
+        y0 = out_max(0, HALF, *terms0)
+        out_round(0, HALF, y0)
+        y2 = out_max(256, P, *terms1)
+        out_round(256, P, y2)
+        y3 = out_max(384, P, *terms1)
+        out_planes(0, HALF)
+        out_round(384, P, y3)
+        out_planes(256, P)
+        out_planes(384, P)
         for q in range(4):
             queue = nc.sync if q % 2 == 0 else nc.scalar
             queue.dma_start(out_2[0][4 * q : 4 * q + 4, :].bitcast(I32), y_plane[32 * q : 32 * q + 4, :].bitcast(I32))

@@ -76,9 +76,15 @@ def tile_picked_ckqgaplerpgmax_none_po_kernel(
         nc.vector.memset(ident[:], 0.0)
         nc.vector.memset(w1s_raw[:].bitcast(I32), 0)
         nc.vector.memset(ds_plane[:].bitcast(I32), 0)
+        b_win = [sb("b_win%d" % t, [P, 2 * N], F32) for t in range(PACK)]
+        s_win = [sb("s_win%d" % c, [P, 2 * N], F32) for c in range(PACK)]
+        for win in b_win:
+            nc.vector.memset(win[:, N:], 0.0)
         nc.gpsimd.dma_start(gain_rows[4:8, :].rearrange("t (b j) -> t b j", j=8), gb.rearrange("(b t j) o -> t b (j o)", t=PACK, j=8))
         nc.gpsimd.dma_start(gain_rows[0:4, :].rearrange("t (b j) -> t b j", j=8), ga.rearrange("(b t j) o -> t b (j o)", t=PACK, j=8))
         make_identity(nc, ident[:], nomemset=True)
+        for win in s_win:
+            nc.gpsimd.memset(win[:, N:], 0.0)
 
         xw_table = sb("xw_table", [P, T], I32)
         dw_table = sb("dw_table", [P, G], I32)
@@ -120,8 +126,8 @@ def tile_picked_ckqgaplerpgmax_none_po_kernel(
         n7_t = load_list("n7_t", n7)
         w1w = sb("w1w", [P, N // 2], I32)
         w1s = sb("w1s", [P, N], U8)
-        deal(nc.vector, w1w[:], w1w_raw[:], 4)
-        deal(nc.vector, w1s[:].bitcast(I32), w1s_raw[:].bitcast(I32), 2)
+        deal(nc.gpsimd, w1w[:], w1w_raw[:], 4)
+        deal(nc.gpsimd, w1s[:].bitcast(I32), w1s_raw[:].bitcast(I32), 2)
 
         b_acc = []
         for t in range(PACK):
@@ -135,11 +141,10 @@ def tile_picked_ckqgaplerpgmax_none_po_kernel(
                 start=True, stop=True,
             )
             b_acc.append(acc)
-        b_win = [sb("b_win%d" % t, [P, N], F32) for t in range(PACK)]
 
         gain_ps = bank(7, "gain_ps")
         nc.tensor.transpose(gain_ps[:, 0:P], gain_rows[:], ident[:])
-        ga16 = keep.tile([P, PACK], F32, name="ga16", tag="terms2", align_bytes=64)
+        ga16 = keep.tile([P, PACK], F32, name="ga16", tag="terms3", align_bytes=64)
         gb_pos = sb("gb_pos", [P, PACK], F32)
         gb_neg = sb("gb_neg", [P, PACK], F32)
         nc.scalar.activation(gb_pos[:], gain_ps[:, 4:8], ACT.Copy)
@@ -153,110 +158,26 @@ def tile_picked_ckqgaplerpgmax_none_po_kernel(
         k1_wd = sb("k1_wd", [P, N], I32)
         deal(nc.vector, k1_wd[:], k1_w[:], 8)
 
-        z2_bf = sb("z2_bf", [P, N * PACK], BF16)
+        z2_bf = keep.tile([P, N * PACK], BF16, name="z2_bf", tag="z2_bf", align_bytes=64)
         z2_codes = sb("z2_codes", [P, N], I32)
         z2_plane = sb("z2_plane", [P, N], U8)
-        z_bf = sb("z_bf", [P, N * PACK], BF16)
         z_codes = sb("z_codes", [P, N], I32)
         z_plane = sb("z_plane", [P, N], U8)
 
-        def b_take(first, t, gate, tag):
-            take = keep.tile([P, HALF], F32, name="take%d_%d" % (first, t), tag=tag, align_bytes=64)
+        rest_part = sb("rest_part", [P, PACK, N], F32)
+        take_part = sb("take_part", [P, PACK, N], F32)
+        for t in range(PACK):
+            nc.scalar.activation(b_win[t][:, 0:N], b_acc[t][:], ACT.Copy)
+            gate = sb("gate%d" % t, [P, N], F32)
+            rest = sb("rest%d" % t, [P, N], F32)
+            take = sb("take%d" % t, [P, N], F32)
+            nc.scalar.activation(gate[:], b_win[t][:].indirect(n4_t[:]), ACT.Sigmoid)
+            nc.scalar.activation(rest[:], gate[:], ACT.Identity, scale=gb_neg[:, t : t + 1], bias=gb_pos[:, t : t + 1])
             nc.scalar.activation(take[:], gate[:], ACT.Copy, scale=gb_pos[:, t : t + 1])
-            return take
+            nc.vector.tensor_tensor(rest_part[:, t, :], b_win[t][:].indirect(n3_t[:]), rest[:], ALU.mult)
+            nc.vector.tensor_tensor(take_part[:, t, :], b_win[t][:].indirect(n5_t[:]), take[:], ALU.mult)
+        summed = [bank(k, "sum%d" % k) for k in range(PACK)]
 
-        def b_gates(first, count):
-            made = []
-            for t in range(PACK):
-                if first == 0:
-                    nc.scalar.activation(b_win[t][:], b_acc[t][:], ACT.Copy)
-                gate = sb("gate%d_%d" % (first, t), [P, count], F32)
-                rest = sb("rest%d_%d" % (first, t), [P, count], F32)
-                nc.scalar.activation(gate[:], b_win[t][:].indirect(entries(n4_t, first, count)), ACT.Sigmoid)
-                nc.scalar.activation(rest[:], gate[:], ACT.Identity, scale=gb_neg[:, t : t + 1], bias=gb_pos[:, t : t + 1])
-                if first == HALF and t == PACK - 1:
-                    made.append((rest, gate))
-                    continue
-                made.append((rest, b_take(first, t, gate, "take%d_%d" % (first, t))))
-            return made
-
-        def terms(tag, name, count):
-            both = keep.tile([P, 2, PACK, count], F32, name="terms_" + name, tag="terms" + tag, align_bytes=64)
-            return both[:, 0, :, :], both[:, 1, :, :]
-
-        def b_terms(tag, first, count, gates):
-            left, right = terms(tag, "b%d" % first, count)
-            for t, (rest, take) in enumerate(gates):
-                nc.vector.tensor_tensor(left[:, t, :], b_win[t][:].indirect(entries(n3_t, first, count)), rest[:], ALU.mult)
-                if first == HALF and t == PACK - 1:
-                    take = b_take(first, t, take, "rounded_a%d_1" % HALF)
-                    quantize_z()
-                nc.vector.tensor_tensor(right[:, t, :], b_win[t][:].indirect(entries(n5_t, first, count)), take[:], ALU.mult)
-            return left, right
-
-        def a_terms(tag, first, count):
-            left, right = terms(tag, "a%d" % first, count)
-            for t in range(PACK):
-                nc.vector.tensor_copy(left[:, t, :], a_win[t][:].indirect(entries(n1_t, first, count)))
-                nc.vector.tensor_scalar(right[:, t, :], a_win[t][:].indirect(entries(n2_t, first, count)), -1.0, 0.0, ALU.mult, ALU.add)
-            return left, right
-
-        def add_and_round(name, left, right, count, bank0):
-            chunks = count // P
-            back = bank(2 + turn[0] % 2, "back_" + name)
-            turn[0] = turn[0] + 1
-            for k in range(chunks):
-                cols = slice(P * k, P * (k + 1))
-                summed = bank(bank0 + k, "sum_%s_%d" % (name, k))
-                for t in range(PACK):
-                    dst = summed[:, P * t : P * (t + 1)]
-                    nc.tensor.matmul(dst, left[:, t, cols], ident[:], start=True, stop=False, is_transpose=True)
-                    nc.tensor.matmul(dst, right[:, t, cols], ident[:], start=False, stop=True, is_transpose=True)
-                rounded = keep.tile([P, N], BF16, name="rounded", tag="rounded_%s_%d" % (name, k), align_bytes=64)
-                nc.scalar.copy(
-                    rounded[:].rearrange("v (u p e) -> v u p e", u=2, e=2),
-                    summed[:].rearrange("v (u e p) -> v u p e", u=2, e=2),
-                )
-                for u in range(2):
-                    nc.tensor.transpose(
-                        back[:, P * (2 * k + u) : P * (2 * k + u + 1)],
-                        rounded[:].bitcast(F32)[:, P * u : P * (u + 1)],
-                        ident[:],
-                    )
-            return back[:, 0 : 2 * count].rearrange("p (k u v) -> p k u v", u=2, v=P)
-
-        def quantize_z2(first, count):
-            nc.vector.quantize_mx(
-                out=z2_codes[:, first : first + count].bitcast(FP8X4),
-                scales=z2_plane[:, first : first + count],
-                in_=z2_bf[:, PACK * first : PACK * (first + count)],
-            )
-
-        def b_finish(first, count, left, right):
-            back = add_and_round("b%d" % first, left, right, count, 0)
-            words = z2_bf[:].bitcast(F32)[:, 2 * first : 2 * (first + count)]
-            nc.scalar.copy(words.rearrange("p (k v u) -> p k v u", u=2, v=P), back.rearrange("p k u v -> p k v u"))
-            quantize_z2(first, count)
-
-        def a_finish(first, count, left, right):
-            back = add_and_round("a%d" % first, left, right, count, 4 if first == 0 else 0)
-            words = z_bf[:].bitcast(F32).rearrange("p (c m u) -> p m c u", c=PACK, u=2)
-            per = P // PACK
-            for k in range(count // P):
-                m0 = first // PACK + per * k
-                nc.scalar.copy(words[:, m0 : m0 + per, :, :], back[:, k, :, :].rearrange("p u (m c) -> p m c u", c=PACK))
-
-        def quantize_z():
-            for c in range(PACK):
-                nc.vector.quantize_mx(
-                    out=z_codes[:, P * c : P * (c + 1)].bitcast(FP8X4),
-                    scales=z_plane[:, P * c : P * (c + 1)],
-                    in_=z_bf[:, N * c : N * (c + 1)],
-                )
-
-        turn = [0]
-        gates0 = b_gates(0, HALF)
-        b0 = b_terms("0", 0, HALF, gates0)
         a_win = []
         for t in range(PACK):
             acc = bank(PACK + t, "a_ps%d" % t)
@@ -271,49 +192,76 @@ def tile_picked_ckqgaplerpgmax_none_po_kernel(
             win = sb("a_win%d" % t, [P, N], F32)
             nc.scalar.activation(win[:], acc[:], ACT.Copy, scale=ga16[:, t : t + 1])
             a_win.append(win)
-        gates1 = b_gates(HALF, HALF)
-        a0 = a_terms("1", 0, HALF)
-        b_finish(0, HALF, *b0)
-        a1 = a_terms("2", HALF, HALF)
-        a_finish(0, HALF, *a0)
-        a_finish(HALF, HALF, *a1)
-        b1 = b_terms("1", HALF, HALF, gates1)
 
-        s_acc = [bank(PACK + c, "s_ps%d" % c) for c in range(PACK)]
-        s_win = [sb("s_win%d" % c, [P, N], F32) for c in range(PACK)]
+        for t in range(PACK):
+            for k in range(PACK):
+                dst = summed[k][:, P * t : P * (t + 1)]
+                cols = slice(P * k, P * (k + 1))
+                nc.tensor.matmul(dst, rest_part[:, t, cols], ident[:], start=True, stop=False, is_transpose=True)
+                nc.tensor.matmul(dst, take_part[:, t, cols], ident[:], start=False, stop=True, is_transpose=True)
 
-        def s_product(c, first, count):
-            rows = slice(P * c, P * (c + 1))
-            cols = slice(first, first + count)
-            nc.tensor.matmul_mx(
-                out=s_acc[c][:, cols],
-                lhsT=z_codes[:, rows].bitcast(FP8X4),
-                lhsT_scale=z_plane[:, rows],
-                rhs=z2_codes[:, cols].bitcast(FP8X4),
-                rhs_scale=z2_plane[:, cols],
-                start=True, stop=True,
-            )
+        def a_diff(first, tag):
+            both = keep.tile([P, 2, PACK, HALF], F32, name="diff%d" % first, tag=tag, align_bytes=64)
+            for t in range(PACK):
+                nc.vector.tensor_copy(both[:, 0, t, :], a_win[t][:].indirect(entries(n2_t, first, HALF)))
+            for t in range(PACK):
+                nc.vector.tensor_tensor(both[:, 1, t, :], a_win[t][:].indirect(entries(n1_t, first, HALF)), both[:, 0, t, :], ALU.subtract)
+            return both[:, 1, :, :].rearrange("p t (m c) -> p m t c", c=PACK)
 
+        def b_finish(first):
+            back = bank(PACK + first // HALF, "back%d" % first)
+            for k in range(2):
+                rounded = keep.tile([P, N], BF16, name="rounded", tag="rounded%d_%d" % (first, k), align_bytes=64)
+                nc.scalar.copy(
+                    rounded[:].rearrange("v (u p e) -> v u p e", u=2, e=2),
+                    summed[first // P + k][:].rearrange("v (u e p) -> v u p e", u=2, e=2),
+                )
+                for u in range(2):
+                    nc.tensor.transpose(
+                        back[:, P * (2 * k + u) : P * (2 * k + u + 1)],
+                        rounded[:].bitcast(F32)[:, P * u : P * (u + 1)],
+                        ident[:],
+                    )
+            words = z2_bf[:].bitcast(F32)[:, 2 * first : 2 * (first + HALF)]
+            nc.scalar.copy(words.rearrange("p (k v u) -> p k v u", u=2, v=P), back[:].rearrange("p (k u v) -> p k v u", u=2, v=P))
+
+        low = a_diff(0, "terms3")
+        b_finish(0)
+        b_finish(HALF)
+        nc.vector.quantize_mx(out=z2_codes[:].bitcast(FP8X4), scales=z2_plane[:], in_=z2_bf[:])
+        z_bf = keep.tile([P, N * PACK], BF16, name="z_bf", tag="rounded%d_1" % HALF, align_bytes=64)
+        z_dealt = z_bf[:].rearrange("p (c m t) -> p m t c", c=PACK, t=PACK)
+        nc.scalar.copy(z_dealt[:, 0 : P // 2, :, :], low)
+        high = a_diff(HALF, "z2_bf")
         for c in range(PACK):
-            s_product(c, 0, HALF)
-            nc.scalar.activation(s_win[c][:, 0:HALF], s_acc[c][:, 0:HALF], ACT.Copy, scale=0.0625)
-        for k in range(2):
-            first = HALF + P * k
-            nc.vector.tensor_tensor(
-                z2_bf[:, PACK * first : PACK * (first + P)].rearrange("p (c i t) -> p c t i", i=4, t=PACK),
-                b1[0][:, :, P * k : P * (k + 1)].rearrange("p t (c i) -> p c t i", i=4),
-                b1[1][:, :, P * k : P * (k + 1)].rearrange("p t (c i) -> p c t i", i=4),
-                ALU.add,
-            )
-        quantize_z2(256, P)
-        quantize_z2(384, P)
-        for c in range(PACK):
-            s_product(c, 256, P)
-            s_product(c, 384, P)
-            if c == 0:
-                nc.vector.tensor_scalar(s_win[c][:, HALF:], s_acc[c][:, HALF:], 0.0625, None, ALU.mult)
+            if c < 2:
+                nc.vector.tensor_copy(z_dealt[:, P // 2 :, :, c], high[:, :, :, c])
             else:
-                nc.scalar.activation(s_win[c][:, HALF:], s_acc[c][:, HALF:], ACT.Copy, scale=0.0625)
+                nc.scalar.copy(z_dealt[:, P // 2 :, :, c], high[:, :, :, c])
+
+        for c in range(PACK):
+            rows = slice(P * c, P * (c + 1))
+            nc.vector.quantize_mx(
+                out=z_codes[:, rows].bitcast(FP8X4),
+                scales=z_plane[:, rows],
+                in_=z_bf[:, N * c : N * (c + 1)],
+            )
+            pieces = ((0, HALF, 0), (HALF, HALF, 1)) if c == 0 else ((0, N, 1 + c),)
+            for first, count, where in pieces:
+                cols = slice(first, first + count)
+                acc = bank(where, "s_ps%d_%d" % (c, first))
+                nc.tensor.matmul_mx(
+                    out=acc[:, 0:count],
+                    lhsT=z_codes[:, rows].bitcast(FP8X4),
+                    lhsT_scale=z_plane[:, rows],
+                    rhs=z2_codes[:, cols].bitcast(FP8X4),
+                    rhs_scale=z2_plane[:, cols],
+                    start=True, stop=True,
+                )
+                if (c == 0 and first > 0) or c == 1:
+                    nc.vector.tensor_scalar(s_win[c][:, cols], acc[:, 0:count], 0.0625, None, ALU.mult)
+                else:
+                    nc.scalar.activation(s_win[c][:, cols], acc[:, 0:count], ACT.Copy, scale=0.0625)
 
         y_bf = sb("y_bf", [P, N, PACK], BF16)
         y_codes = sb("y_codes", [P, N], I32)
@@ -321,22 +269,25 @@ def tile_picked_ckqgaplerpgmax_none_po_kernel(
         out_rows = out_0.rearrange("(m c) v -> m c v", c=PACK)
         out_words = out_1[0].rearrange("p n t -> p (n t)").bitcast(I32)
 
+        other = sb("other", [P, PACK, N], F32)
+        for c in range(PACK):
+            nc.vector.tensor_copy(other[:, c, :], s_win[c][:].indirect(n7_t[:]))
+
         def out_terms(first):
             cols = slice(first, first + HALF)
             gate6 = sb("gate6_%d" % first, [P, PACK, HALF], F32)
-            other = sb("other%d" % first, [P, PACK, HALF], F32)
             gated = sb("gated%d" % first, [P, PACK, HALF], F32)
             for c in range(PACK):
                 nc.scalar.activation(gate6[:, c, :], s_win[c][:].indirect(entries(n6_t, first, HALF)), ACT.Sigmoid)
-                nc.vector.tensor_copy(other[:, c, :], s_win[c][:].indirect(entries(n7_t, first, HALF)))
             for c in range(PACK):
-                nc.vector.tensor_tensor(gated[:, c, :], s_win[c][:, cols], gate6[:, c, :], ALU.mult)
-            return gated, other
+                engine = nc.gpsimd if first == 0 or c < 3 else nc.vector
+                engine.tensor_tensor(gated[:, c, :], s_win[c][:, cols], gate6[:, c, :], ALU.mult)
+            return gated, other[:, :, cols]
 
-        def out_max(first, count, gated, other):
+        def out_max(first, count, gated, picked):
             part = slice(first % HALF, first % HALF + count)
             y = sb("y%d" % first, [P, PACK, count], F32)
-            nc.vector.tensor_tensor(y[:], gated[:, :, part], other[:, :, part], ALU.max)
+            nc.vector.tensor_tensor(y[:], gated[:, :, part], picked[:, :, part], ALU.max)
             nc.sync.dma_start(out_rows[:, :, first : first + count], y[:])
             return y
 
@@ -366,8 +317,7 @@ def tile_picked_ckqgaplerpgmax_none_po_kernel(
         y3 = out_max(384, P, *terms1)
         out_planes(0, HALF)
         out_round(384, P, y3)
-        out_planes(256, P)
-        out_planes(384, P)
+        out_planes(HALF, HALF)
         for q in range(4):
             queue = nc.sync if q % 2 == 0 else nc.scalar
             queue.dma_start(out_2[0][4 * q : 4 * q + 4, :].bitcast(I32), y_plane[32 * q : 32 * q + 4, :].bitcast(I32))

@@ -77,14 +77,15 @@ def tile_picked_ckqgaplerpgmax_none_po_kernel(
         nc.vector.memset(w1s_raw[:].bitcast(I32), 0)
         nc.vector.memset(ds_plane[:].bitcast(I32), 0)
         b_win = [sb("b_win%d" % t, [P, 2 * N], F32) for t in range(PACK)]
-        s_win = [sb("s_win%d" % c, [P, 2 * N], F32) for c in range(PACK)]
+        a_win = [sb("a_win%d" % t, [P, 2 * N], F32) for t in range(PACK)]
+        s_win = b_win
         for win in b_win:
             nc.vector.memset(win[:, N:], 0.0)
         nc.gpsimd.dma_start(gain_rows[4:8, :].rearrange("t (b j) -> t b j", j=8), gb.rearrange("(b t j) o -> t b (j o)", t=PACK, j=8))
         nc.gpsimd.dma_start(gain_rows[0:4, :].rearrange("t (b j) -> t b j", j=8), ga.rearrange("(b t j) o -> t b (j o)", t=PACK, j=8))
         make_identity(nc, ident[:], nomemset=True)
-        for win in s_win:
-            nc.gpsimd.memset(win[:, N:], 0.0)
+        for t in range(PACK):
+            nc.scalar.copy(a_win[t][:, N:], b_win[t][:, N:])
 
         xw_table = sb("xw_table", [P, T], I32)
         dw_table = sb("dw_table", [P, G], I32)
@@ -144,7 +145,7 @@ def tile_picked_ckqgaplerpgmax_none_po_kernel(
 
         gain_ps = bank(7, "gain_ps")
         nc.tensor.transpose(gain_ps[:, 0:P], gain_rows[:], ident[:])
-        ga16 = keep.tile([P, PACK], F32, name="ga16", tag="terms3", align_bytes=64)
+        ga16 = sb("ga16", [P, PACK], F32)
         gb_pos = sb("gb_pos", [P, PACK], F32)
         gb_neg = sb("gb_neg", [P, PACK], F32)
         nc.scalar.activation(gb_pos[:], gain_ps[:, 4:8], ACT.Copy)
@@ -158,7 +159,7 @@ def tile_picked_ckqgaplerpgmax_none_po_kernel(
         k1_wd = sb("k1_wd", [P, N], I32)
         deal(nc.vector, k1_wd[:], k1_w[:], 8)
 
-        z2_bf = keep.tile([P, N * PACK], BF16, name="z2_bf", tag="z2_bf", align_bytes=64)
+        z2_bf = sb("z2_bf", [P, N * PACK], BF16)
         z2_codes = sb("z2_codes", [P, N], I32)
         z2_plane = sb("z2_plane", [P, N], U8)
         z_codes = sb("z_codes", [P, N], I32)
@@ -174,11 +175,13 @@ def tile_picked_ckqgaplerpgmax_none_po_kernel(
             nc.scalar.activation(gate[:], b_win[t][:].indirect(n4_t[:]), ACT.Sigmoid)
             nc.scalar.activation(rest[:], gate[:], ACT.Identity, scale=gb_neg[:, t : t + 1], bias=gb_pos[:, t : t + 1])
             nc.scalar.activation(take[:], gate[:], ACT.Copy, scale=gb_pos[:, t : t + 1])
-            nc.vector.tensor_tensor(rest_part[:, t, :], b_win[t][:].indirect(n3_t[:]), rest[:], ALU.mult)
-            nc.vector.tensor_tensor(take_part[:, t, :], b_win[t][:].indirect(n5_t[:]), take[:], ALU.mult)
-        summed = [bank(k, "sum%d" % k) for k in range(PACK)]
+            at3 = sb("at3_%d" % t, [P, N], F32)
+            at5 = sb("at5_%d" % t, [P, N], F32)
+            nc.vector.tensor_copy(at3[:], b_win[t][:].indirect(n3_t[:]))
+            nc.vector.tensor_copy(at5[:], b_win[t][:].indirect(n5_t[:]))
+            nc.gpsimd.tensor_tensor(rest_part[:, t, :], at3[:], rest[:], ALU.mult)
+            nc.gpsimd.tensor_tensor(take_part[:, t, :], at5[:], take[:], ALU.mult)
 
-        a_win = []
         for t in range(PACK):
             acc = bank(PACK + t, "a_ps%d" % t)
             nc.tensor.matmul_mx(
@@ -189,10 +192,9 @@ def tile_picked_ckqgaplerpgmax_none_po_kernel(
                 rhs_scale=offs_s[:],
                 start=True, stop=True,
             )
-            win = sb("a_win%d" % t, [P, N], F32)
-            nc.scalar.activation(win[:], acc[:], ACT.Copy, scale=ga16[:, t : t + 1])
-            a_win.append(win)
+            nc.scalar.activation(a_win[t][:, 0:N], acc[:], ACT.Copy, scale=ga16[:, t : t + 1])
 
+        summed = [bank(k, "sum%d" % k) for k in range(PACK)]
         for t in range(PACK):
             for k in range(PACK):
                 dst = summed[k][:, P * t : P * (t + 1)]
@@ -200,13 +202,19 @@ def tile_picked_ckqgaplerpgmax_none_po_kernel(
                 nc.tensor.matmul(dst, rest_part[:, t, cols], ident[:], start=True, stop=False, is_transpose=True)
                 nc.tensor.matmul(dst, take_part[:, t, cols], ident[:], start=False, stop=True, is_transpose=True)
 
-        def a_diff(first, tag):
-            both = keep.tile([P, 2, PACK, HALF], F32, name="diff%d" % first, tag=tag, align_bytes=64)
-            for t in range(PACK):
-                nc.vector.tensor_copy(both[:, 0, t, :], a_win[t][:].indirect(entries(n2_t, first, HALF)))
-            for t in range(PACK):
-                nc.vector.tensor_tensor(both[:, 1, t, :], a_win[t][:].indirect(entries(n1_t, first, HALF)), both[:, 0, t, :], ALU.subtract)
-            return both[:, 1, :, :].rearrange("p t (m c) -> p m t c", c=PACK)
+        diff = sb("diff", [P, PACK, N], F32)
+        for t in range(PACK):
+            at2 = sb("at2_%d" % t, [P, N], F32)
+            nc.vector.tensor_copy(at2[:], a_win[t][:].indirect(n2_t[:]))
+            if t < PACK - 1:
+                at1 = sb("at1_%d" % t, [P, N], F32)
+                nc.vector.tensor_copy(at1[:], a_win[t][:].indirect(n1_t[:]))
+                nc.gpsimd.tensor_tensor(diff[:, t, :], at1[:], at2[:], ALU.subtract)
+            else:
+                for first in (0, HALF):
+                    cols = slice(first, first + HALF)
+                    nc.vector.tensor_tensor(diff[:, t, cols], a_win[t][:].indirect(entries(n1_t, first, HALF)), at2[:, cols], ALU.subtract)
+        z_f32 = diff[:].rearrange("p t (m c) -> p m t c", c=PACK)
 
         def b_finish(first):
             back = bank(PACK + first // HALF, "back%d" % first)
@@ -225,19 +233,14 @@ def tile_picked_ckqgaplerpgmax_none_po_kernel(
             words = z2_bf[:].bitcast(F32)[:, 2 * first : 2 * (first + HALF)]
             nc.scalar.copy(words.rearrange("p (k v u) -> p k v u", u=2, v=P), back[:].rearrange("p (k u v) -> p k v u", u=2, v=P))
 
-        low = a_diff(0, "terms3")
         b_finish(0)
         b_finish(HALF)
-        nc.vector.quantize_mx(out=z2_codes[:].bitcast(FP8X4), scales=z2_plane[:], in_=z2_bf[:])
         z_bf = keep.tile([P, N * PACK], BF16, name="z_bf", tag="rounded%d_1" % HALF, align_bytes=64)
         z_dealt = z_bf[:].rearrange("p (c m t) -> p m t c", c=PACK, t=PACK)
-        nc.scalar.copy(z_dealt[:, 0 : P // 2, :, :], low)
-        high = a_diff(HALF, "z2_bf")
-        for c in range(PACK):
-            if c < 2:
-                nc.vector.tensor_copy(z_dealt[:, P // 2 :, :, c], high[:, :, :, c])
-            else:
-                nc.scalar.copy(z_dealt[:, P // 2 :, :, c], high[:, :, :, c])
+        nc.scalar.copy(z_dealt[:, :, 0:2, :], z_f32[:, :, 0:2, :])
+        nc.scalar.copy(z_dealt[:, 0 : P // 2, 2:4, :], z_f32[:, 0 : P // 2, 2:4, :])
+        nc.scalar.copy(z_dealt[:, P // 2 :, 2:4, :], z_f32[:, P // 2 :, 2:4, :])
+        nc.vector.quantize_mx(out=z2_codes[:].bitcast(FP8X4), scales=z2_plane[:], in_=z2_bf[:])
 
         for c in range(PACK):
             rows = slice(P * c, P * (c + 1))

from contextlib import ExitStack

import concourse.mybir as mybir
from concourse.masks import make_identity

F32 = mybir.dt.float32
BF16 = mybir.dt.bfloat16
I32 = mybir.dt.int32
U32 = mybir.dt.uint32
U16 = mybir.dt.uint16
U8 = mybir.dt.uint8
FP8X4 = mybir.dt.float8_e4m3fn_x4
FP4X4 = mybir.dt.float4_e2m1fn_x4
ACT = mybir.ActivationFunctionType
ALU = mybir.AluOpType

P = 128
PACK = 4
N = 512
T = 1024
G = 2048
HALF = N // 2
LANES = 16
OUT_SLICES = ((0, 256), (256, 128), (384, 128))
FLOPS = 3 * 2 * 512 * 512 * 512


def entries(offsets, first, count):
    return offsets[:, first // LANES : (first + count) // LANES]


def deal(engine, dst, src, run):
    engine.tensor_copy(
        out=dst.rearrange("p (t b j) -> p t b j", t=PACK, j=run),
        in_=src.rearrange("p (b t j) -> p t b j", t=PACK, j=run),
    )


def tile_picked_ckqgaplerpgmax_none_po_kernel(
    tc, x_words, x_scales, d_words, d_scales, w1_words, w1_scales, ga, gb,
    offs, k1, two, n1, n2, n3, n4, n5, n6, n7, out_0, out_1, out_2,
):
    nc = tc.nc
    with ExitStack() as ctx:
        lists = ctx.enter_context(tc.tile_pool(name="lists", bufs=1))
        keep = ctx.enter_context(tc.tile_pool(name="keep", bufs=1))
        psum = ctx.enter_context(tc.psum_pool(name="psum", bufs=1))

        def sb(name, shape, dtype):
            return keep.tile(shape, dtype, name=name, align_bytes=64)

        def bank(i, name):
            return psum.tile([P, N], F32, name=name, tag="bank%d" % i)

        def load_list(name, src):
            tile = lists.tile([P, N // LANES], U16, name=name)
            nc.sync.dma_start(tile[:], src)
            return tile

        def load_scale_rows(queue, plane, rows):
            for q in range(4):
                queue.dma_start(plane[32 * q : 32 * q + 4, :].bitcast(I32), rows[4 * q : 4 * q + 4, :].bitcast(I32))

        xs_table = sb("xs_table", [P, T], U8)
        ds_table = sb("ds_table", [P, G], U8)
        w1s_raw = sb("w1s_raw", [P, N], U8)
        ds_plane = sb("ds_plane", [P, N], U8)
        gain_rows = sb("gain_rows", [P, P], F32)
        ident = sb("ident", [P, P], F32)
        warm = sb("warm", [P, 2], F32)
        nc.gpsimd.memset(xs_table[:].bitcast(I32), 0)
        nc.gpsimd.memset(warm[:], 0.0)
        nc.scalar.activation(warm[:, 1:2], warm[:, 0:1], ACT.Sigmoid)
        nc.vector.memset(gain_rows[:], 0.0)
        nc.vector.memset(ds_table[:].bitcast(I32), 0)
        nc.vector.memset(ident[:], 0.0)
        nc.vector.memset(w1s_raw[:].bitcast(I32), 0)
        nc.vector.memset(ds_plane[:].bitcast(I32), 0)
        b_win = [sb("b_win%d" % t, [P, 2 * N], F32) for t in range(PACK)]
        a_win = [sb("a_win%d" % t, [P, 2 * N], F32) for t in range(PACK)]
        s_win = b_win
        for win in b_win:
            nc.vector.memset(win[:, N:], 0.0)
        nc.gpsimd.dma_start(gain_rows[4:8, :].rearrange("t (b j) -> t b j", j=8), gb.rearrange("(b t j) o -> t b (j o)", t=PACK, j=8))
        nc.gpsimd.dma_start(gain_rows[0:4, :].rearrange("t (b j) -> t b j", j=8), ga.rearrange("(b t j) o -> t b (j o)", t=PACK, j=8))
        make_identity(nc, ident[:], nomemset=True)
        for t in range(PACK):
            nc.scalar.copy(a_win[t][:, N:], b_win[t][:, N:])

        xw_table = sb("xw_table", [P, T], I32)
        dw_table = sb("dw_table", [P, G], I32)
        w1w_raw = sb("w1w_raw", [P, N // 2], I32)

        two_t = load_list("two_t", two)
        load_scale_rows(nc.sync, xs_table, x_scales[0])
        k1_t = load_list("k1_t", k1)
        nc.sync.dma_start(ds_table[0:P:8, :].bitcast(I32), d_scales[0].bitcast(I32))
        nc.sync.dma_start(xw_table[:], x_words[0].rearrange("p n t -> p (n t)").bitcast(I32))
        nc.sync.dma_start(w1w_raw[:], w1_words[0].bitcast(I32))
        load_scale_rows(nc.sync, w1s_raw, w1_scales[0])
        offs_t = load_list("offs_t", offs)
        n4_t = load_list("n4_t", n4)
        nc.sync.dma_start(dw_table[:], d_words[0].rearrange("p n t -> p (n t)").bitcast(I32))
        n3_t = load_list("n3_t", n3)
        n5_t = load_list("n5_t", n5)

        def gather_words(name, table, offsets):
            picked = sb(name, [P, N], I32)
            nc.vector.tensor_copy(picked[:].bitcast(U32), table[:].bitcast(U32).indirect(offsets[:]))
            return picked

        def gather_bytes(name, table, offsets):
            picked = sb(name, [P, N], U8)
            nc.vector.tensor_copy(picked[:], table[:].indirect(offsets[:]))
            return picked

        two_s = gather_bytes("two_s", xs_table, two_t)
        k1_s = gather_bytes("k1_s", ds_table, k1_t)
        two_w = gather_words("two_w", xw_table, two_t)
        k1_sd = sb("k1_sd", [P, N], U8)
        deal(nc.vector, k1_sd[:].bitcast(I32), k1_s[:].bitcast(I32), 2)
        for q in range(4):
            nc.sync.dma_start(ds_plane[32 * q : 32 * q + 4, :].bitcast(I32), k1_sd[32 * q : 32 * q + 32 : 8, :].bitcast(I32))
        n2_t = load_list("n2_t", n2)
        n1_t = load_list("n1_t", n1)
        n6_t = load_list("n6_t", n6)
        n7_t = load_list("n7_t", n7)
        w1w = sb("w1w", [P, N // 2], I32)
        w1s = sb("w1s", [P, N], U8)
        deal(nc.gpsimd, w1w[:], w1w_raw[:], 4)
        deal(nc.gpsimd, w1s[:].bitcast(I32), w1s_raw[:].bitcast(I32), 2)

        b_acc = []
        for t in range(PACK):
            acc = bank(t, "b_ps%d" % t)
            nc.tensor.matmul_mx(
                out=acc[:],
                lhsT=w1w[:].bitcast(U8)[:, 2 * P * t : 2 * P * (t + 1)].bitcast(FP4X4),
                lhsT_scale=w1s[:, P * t : P * (t + 1)],
                rhs=two_w[:].bitcast(FP8X4),
                rhs_scale=two_s[:],
                start=True, stop=True,
            )
            b_acc.append(acc)

        gain_ps = bank(7, "gain_ps")
        nc.tensor.transpose(gain_ps[:, 0:P], gain_rows[:], ident[:])
        ga16 = sb("ga16", [P, PACK], F32)
        gb_pos = sb("gb_pos", [P, PACK], F32)
        gb_neg = sb("gb_neg", [P, PACK], F32)
        nc.scalar.activation(gb_pos[:], gain_ps[:, 4:8], ACT.Copy)
        nc.scalar.activation(gb_neg[:], gain_ps[:, 4:8], ACT.Copy, scale=-1.0)
        nc.scalar.activation(ga16[:], gain_ps[:, 0:4], ACT.Copy, scale=0.0625)


        offs_s = gather_bytes("offs_s", xs_table, offs_t)
        offs_w = gather_words("offs_w", xw_table, offs_t)
        k1_w = gather_words("k1_w", dw_table, k1_t)
        k1_wd = sb("k1_wd", [P, N], I32)
        deal(nc.vector, k1_wd[:], k1_w[:], 8)

        z2_bf = sb("z2_bf", [P, N * PACK], BF16)
        z2_codes = sb("z2_codes", [P, N], I32)
        z2_plane = sb("z2_plane", [P, N], U8)
        z_codes = sb("z_codes", [P, N], I32)
        z_plane = sb("z_plane", [P, N], U8)

        rest_part = sb("rest_part", [P, PACK, N], F32)
        take_part = sb("take_part", [P, PACK, N], F32)
        for t in range(PACK):
            nc.scalar.activation(b_win[t][:, 0:N], b_acc[t][:], ACT.Copy)
            gate = sb("gate%d" % t, [P, N], F32)
            rest = sb("rest%d" % t, [P, N], F32)
            take = sb("take%d" % t, [P, N], F32)
            nc.scalar.activation(gate[:], b_win[t][:].indirect(n4_t[:]), ACT.Sigmoid)
            nc.scalar.activation(rest[:], gate[:], ACT.Identity, scale=gb_neg[:, t : t + 1], bias=gb_pos[:, t : t + 1])
            nc.scalar.activation(take[:], gate[:], ACT.Copy, scale=gb_pos[:, t : t + 1])
            at3 = sb("at3_%d" % t, [P, N], F32)
            at5 = sb("at5_%d" % t, [P, N], F32)
            nc.vector.tensor_copy(at3[:], b_win[t][:].indirect(n3_t[:]))
            nc.vector.tensor_copy(at5[:], b_win[t][:].indirect(n5_t[:]))
            nc.gpsimd.tensor_tensor(rest_part[:, t, :], at3[:], rest[:], ALU.mult)
            nc.gpsimd.tensor_tensor(take_part[:, t, :], at5[:], take[:], ALU.mult)

        for t in range(PACK):
            acc = bank(PACK + t, "a_ps%d" % t)
            nc.tensor.matmul_mx(
                out=acc[:],
                lhsT=k1_wd[:, P * t : P * (t + 1)].bitcast(FP8X4),
                lhsT_scale=ds_plane[:, P * t : P * (t + 1)],
                rhs=offs_w[:].bitcast(FP8X4),
                rhs_scale=offs_s[:],
                start=True, stop=True,
            )
            nc.scalar.activation(a_win[t][:, 0:N], acc[:], ACT.Copy, scale=ga16[:, t : t + 1])

        summed = [bank(k, "sum%d" % k) for k in range(PACK)]
        for t in range(PACK):
            for k in range(PACK):
                dst = summed[k][:, P * t : P * (t + 1)]
                cols = slice(P * k, P * (k + 1))
                nc.tensor.matmul(dst, rest_part[:, t, cols], ident[:], start=True, stop=False, is_transpose=True)
                nc.tensor.matmul(dst, take_part[:, t, cols], ident[:], start=False, stop=True, is_transpose=True)

        diff = sb("diff", [P, PACK, N], F32)
        for t in range(PACK):
            at2 = sb("at2_%d" % t, [P, N], F32)
            nc.vector.tensor_copy(at2[:], a_win[t][:].indirect(n2_t[:]))
            if t < PACK - 1:
                at1 = sb("at1_%d" % t, [P, N], F32)
                nc.vector.tensor_copy(at1[:], a_win[t][:].indirect(n1_t[:]))
                nc.gpsimd.tensor_tensor(diff[:, t, :], at1[:], at2[:], ALU.subtract)
            else:
                for first in (0, HALF):
                    cols = slice(first, first + HALF)
                    nc.vector.tensor_tensor(diff[:, t, cols], a_win[t][:].indirect(entries(n1_t, first, HALF)), at2[:, cols], ALU.subtract)
        z_f32 = diff[:].rearrange("p t (m c) -> p m t c", c=PACK)

        def b_finish(first):
            back = bank(PACK + first // HALF, "back%d" % first)
            for k in range(2):
                rounded = keep.tile([P, N], BF16, name="rounded", tag="rounded%d_%d" % (first, k), align_bytes=64)
                nc.scalar.copy(
                    rounded[:].rearrange("v (u p e) -> v u p e", u=2, e=2),
                    summed[first // P + k][:].rearrange("v (u e p) -> v u p e", u=2, e=2),
                )
                for u in range(2):
                    nc.tensor.transpose(
                        back[:, P * (2 * k + u) : P * (2 * k + u + 1)],
                        rounded[:].bitcast(F32)[:, P * u : P * (u + 1)],
                        ident[:],
                    )
            words = z2_bf[:].bitcast(F32)[:, 2 * first : 2 * (first + HALF)]
            nc.scalar.copy(words.rearrange("p (k v u) -> p k v u", u=2, v=P), back[:].rearrange("p (k u v) -> p k v u", u=2, v=P))

        b_finish(0)
        b_finish(HALF)
        z_bf = keep.tile([P, N * PACK], BF16, name="z_bf", tag="rounded%d_1" % HALF, align_bytes=64)
        z_dealt = z_bf[:].rearrange("p (c m t) -> p m t c", c=PACK, t=PACK)
        nc.scalar.copy(z_dealt[:, :, 0:2, :], z_f32[:, :, 0:2, :])
        nc.scalar.copy(z_dealt[:, 0 : P // 2, 2:4, :], z_f32[:, 0 : P // 2, 2:4, :])
        nc.scalar.copy(z_dealt[:, P // 2 :, 2:4, :], z_f32[:, P // 2 :, 2:4, :])
        nc.vector.quantize_mx(out=z2_codes[:].bitcast(FP8X4), scales=z2_plane[:], in_=z2_bf[:])

        for c in range(PACK):
            rows = slice(P * c, P * (c + 1))
            nc.vector.quantize_mx(
                out=z_codes[:, rows].bitcast(FP8X4),
                scales=z_plane[:, rows],
                in_=z_bf[:, N * c : N * (c + 1)],
            )
            pieces = ((0, HALF, 0), (HALF, HALF, 1)) if c == 0 else ((0, N, 1 + c),)
            for first, count, where in pieces:
                cols = slice(first, first + count)
                acc = bank(where, "s_ps%d_%d" % (c, first))
                nc.tensor.matmul_mx(
                    out=acc[:, 0:count],
                    lhsT=z_codes[:, rows].bitcast(FP8X4),
                    lhsT_scale=z_plane[:, rows],
                    rhs=z2_codes[:, cols].bitcast(FP8X4),
                    rhs_scale=z2_plane[:, cols],
                    start=True, stop=True,
                )
                if (c == 0 and first > 0) or c == 1:
                    nc.vector.tensor_scalar(s_win[c][:, cols], acc[:, 0:count], 0.0625, None, ALU.mult)
                else:
                    nc.scalar.activation(s_win[c][:, cols], acc[:, 0:count], ACT.Copy, scale=0.0625)

        y_bf = sb("y_bf", [P, N, PACK], BF16)
        y_codes = sb("y_codes", [P, N], I32)
        y_plane = sb("y_plane", [P, N], U8)
        out_rows = out_0.rearrange("(m c) v -> m c v", c=PACK)
        out_words = out_1[0].rearrange("p n t -> p (n t)").bitcast(I32)

        other = sb("other", [P, PACK, N], F32)
        for c in range(PACK):
            nc.vector.tensor_copy(other[:, c, :], s_win[c][:].indirect(n7_t[:]))

        def out_terms(first):
            cols = slice(first, first + HALF)
            gate6 = sb("gate6_%d" % first, [P, PACK, HALF], F32)
            gated = sb("gated%d" % first, [P, PACK, HALF], F32)
            for c in range(PACK):
                nc.scalar.activation(gate6[:, c, :], s_win[c][:].indirect(entries(n6_t, first, HALF)), ACT.Sigmoid)
            for c in range(PACK):
                engine = nc.gpsimd if first == 0 or c < 3 else nc.vector
                engine.tensor_tensor(gated[:, c, :], s_win[c][:, cols], gate6[:, c, :], ALU.mult)
            return gated, other[:, :, cols]

        def out_max(first, count, gated, picked):
            part = slice(first % HALF, first % HALF + count)
            y = sb("y%d" % first, [P, PACK, count], F32)
            nc.vector.tensor_tensor(y[:], gated[:, :, part], picked[:, :, part], ALU.max)
            nc.sync.dma_start(out_rows[:, :, first : first + count], y[:])
            return y

        def out_round(first, count, y):
            dst = y_bf[:, first : first + count, :].rearrange("p (c i) t -> p c t i", i=4)
            src = y[:].rearrange("p t (c i) -> p c t i", i=4)
            if first + count == N:
                nc.vector.tensor_copy(dst, src)
            else:
                nc.scalar.copy(dst, src)

        def out_planes(first, count):
            cols = slice(first, first + count)
            nc.vector.quantize_mx(
                out=y_codes[:, cols].bitcast(FP8X4),
                scales=y_plane[:, cols],
                in_=y_bf[:, cols, :].rearrange("p v t -> p (v t)"),
            )
            nc.sync.dma_start(out_words[:, cols], y_codes[:, cols])

        terms0 = out_terms(0)
        terms1 = out_terms(HALF)
        y0 = out_max(0, HALF, *terms0)
        out_round(0, HALF, y0)
        y2 = out_max(256, P, *terms1)
        out_round(256, P, y2)
        y3 = out_max(384, P, *terms1)
        out_planes(0, HALF)
        out_round(384, P, y3)
        out_planes(HALF, HALF)
        for q in range(4):
            queue = nc.sync if q % 2 == 0 else nc.scalar
            queue.dma_start(out_2[0][4 * q : 4 * q + 4, :].bitcast(I32), y_plane[32 * q : 32 * q + 4, :].bitcast(I32))
